import numpy as np
import ml_dtypes


def mxq(x, axis, fmt="e4m3"):
    dtype, down = {"e4m3": (ml_dtypes.float8_e4m3fn, 7), "e5m2": (ml_dtypes.float8_e5m2, 14)}[fmt]
    v = np.moveaxis(np.asarray(x, np.float32).astype(ml_dtypes.bfloat16).astype(np.float64), axis, -1)
    blocks = v.reshape(v.shape[:-1] + (-1, 32))
    amax = np.abs(blocks).max(-1, keepdims=True)
    byte = np.maximum(np.where(amax > 0, np.frexp(amax)[1] - 1 + 127, 0) - down, 1)
    scale = np.exp2(byte - 127.0)
    codes = (blocks / scale).astype(np.float32).astype(dtype).astype(np.float64)
    return np.moveaxis((codes * scale).reshape(v.shape), -1, axis)


WIDE = False


def mx_kscale(k):
    if not WIDE:
        return np.ones(k)
    levels = np.array([10, -10, 5, -5, 0])
    if k % 512:
        return np.exp2(np.random.permutation(np.resize(levels, k // 32))).repeat(32)
    a = np.empty((k // 512, 16))
    for p in range(k // 512):
        a[p, :8] = np.random.permutation(np.resize(levels, 8))
        for g in range(8):
            far = levels[np.abs(levels - a[p, g]) >= 10]
            a[p, g + 8] = far[np.random.randint(len(far))]
    return np.exp2(a.ravel()).repeat(32)


def f64(x):
    return np.asarray(x).astype(np.float64)


def striped(idx):
    return np.tile(idx.reshape(-1, 16).T, (8, 1)).astype(np.uint16)


def unstriped(offs):
    return offs[:16].T.reshape(-1).astype(np.int64)


def striped8(idx):
    return np.concatenate([x.reshape(-1, 16).T for x in idx]).astype(np.uint16)


def runs(offs, k):
    lists = np.stack([offs[16 * r : 16 * r + 16].T.reshape(-1) for r in range(8)]).astype(np.int64)
    return lists[np.arange(k) % 512 // 64]


def pack_weight(w):
    k, n = w.shape
    w = f64(np.asarray(w, np.float32).astype(ml_dtypes.bfloat16)).reshape(k // 32, 32, n)
    amax = np.abs(w).max(1)
    byte = np.clip(np.where(amax > 0, np.frexp(amax)[1] - 1 + 127 - 7, 1), 1, 254)
    scaled = (w * np.exp2(127.0 - byte)[:, None, :]).reshape(k, n).astype(np.float32)
    words = np.ascontiguousarray(scaled.reshape(k // 512, 128, 4, n).transpose(0, 1, 3, 2)).astype(ml_dtypes.float8_e4m3fn).view(np.uint8)
    return words, np.ascontiguousarray(byte.astype(np.uint8).reshape(k // 512, 16, n))


def unpack_weight(words, scales):
    g, p, n, _ = words.shape
    vals = np.ascontiguousarray(words).view(ml_dtypes.float8_e4m3fn).astype(np.float64) * np.repeat(np.exp2(scales.astype(np.float64) - 127.0), 8, axis=1)[..., None]
    return vals.transpose(0, 1, 3, 2).reshape(g * 512, n)


K, T, S, H, C = 512, 2048, 512, 512, 512


def setup_inputs():
    n = np.random.standard_normal
    s = mx_kscale(K)[:, None]
    packed_xT = pack_weight(n((K, T)) * s)
    return {
        "x_words": packed_xT[0],
        "x_scales": packed_xT[1],
        "w1": (n((K, H)) / np.sqrt(K) / s).astype(np.float32),
        "gs": (np.random.uniform(0.5, 1.5, (K, 1)) / s).astype(np.float32),
        "offs": striped(np.random.permutation(T)[:S]),
        "n1": striped8(np.stack([np.random.permutation(S) for _ in range(8)])),
        "n2": striped8(np.stack([np.random.permutation(S) for _ in range(8)])),
        "n3": striped8(np.stack([np.random.permutation(S) for _ in range(8)])),
        "n4": striped8(np.stack([np.random.permutation(S) for _ in range(8)])),
        "cand": striped(np.random.permutation(T)[:C]),
        "n5": striped8(np.stack([np.random.permutation(S) for _ in range(8)])),
        "n6": striped8(np.stack([np.random.permutation(S) for _ in range(8)])),
    }


def reference(x_words, x_scales, w1, gs, offs, n1, n2, n3, n4, cand, n5, n6):
    x_cand = unpack_weight(x_words, x_scales)[:, unstriped(cand)]
    xq = unpack_weight(x_words, x_scales)[:, unstriped(offs)]
    y = mxq(f64(w1), 0, "e4m3").T @ xq
    z = f64(gs) * (0.75 * ((y[np.arange(H)[:, None], runs(n1, H)]) * (y[np.arange(H)[:, None], runs(n2, H)]) - ((y[np.arange(H)[:, None], runs(n3, H)]) * (y[np.arange(H)[:, None], runs(n4, H)]))))
    s = 0.0625 * ((x_cand.T @ mxq(z, 0, "e4m3")))
    st = s + 0.5 * (s[np.arange(C)[:, None], runs(n5, C)])
    return st - (st[np.arange(C)[:, None], runs(n6, C)])

@@ -1,0 +1,186 @@
+from contextlib import ExitStack
+
+import concourse.mybir as mybir
+
+K, T, S, H, C = 512, 2048, 512, 512, 512
+FLOPS = 2 * K * H * S + 2 * K * C * S
+
+F32 = mybir.dt.float32
+BF16 = mybir.dt.bfloat16
+I32 = mybir.dt.int32
+U32 = mybir.dt.uint32
+U16 = mybir.dt.uint16
+U8 = mybir.dt.uint8
+FP8X4 = mybir.dt.float8_e4m3fn_x4
+MULT = mybir.AluOpType.mult
+ADD = mybir.AluOpType.add
+SUBTRACT = mybir.AluOpType.subtract
+COPY = mybir.ActivationFunctionType.Copy
+
+P = 128
+PACK = 4
+WINDOW = 2 * S
+Z_CHUNKS = ((0, 256), (256, 384), (384, 512))
+
+
+def tile_picked_canddethop_none_p_kernel(
+    tc, x_words, x_scales, w1, gs, offs, n1, n2, n3, n4, cand, n5, n6, out
+):
+    nc = tc.nc
+    with ExitStack() as ctx:
+        keep = ctx.enter_context(tc.tile_pool(name="keep", bufs=1))
+        psum = ctx.enter_context(tc.psum_pool(name="psum", bufs=4))
+        psum_first = ctx.enter_context(tc.psum_pool(name="psum_first", bufs=1))
+
+        def load_list(name, source):
+            tile = keep.tile([P, S // 16], U16, name=name)
+            nc.sync.dma_start(tile[:], source)
+            return tile
+
+        table_scales = keep.tile([P, T], U8, name="table_scales", align_bytes=64)
+        nc.vector.memset(table_scales[:].bitcast(I32), 0)
+        offs_sb = load_list("offs_sb", offs)
+        for q in range(4):
+            nc.sync.dma_start(
+                table_scales[32 * q : 32 * q + 4, :].bitcast(I32),
+                x_scales[0, 4 * q : 4 * q + 4, :].bitcast(I32),
+            )
+        cand_sb = load_list("cand_sb", cand)
+        w_rows = w1.rearrange("(p j) c -> p j c", j=PACK)
+        w_raw = []
+        for u in range(2):
+            half = keep.tile([P, PACK, H // 2], F32, name=f"w_raw{u}")
+            nc.sync.dma_start(half[:], w_rows[:, :, u * (H // 2) : (u + 1) * (H // 2)])
+            w_raw.append(half)
+        table_words = keep.tile([P, T], U32, name="table_words", align_bytes=64)
+        nc.sync.dma_start(table_words[:].bitcast(I32), x_words[0].rearrange("p n t -> p (n t)").bitcast(I32))
+        gs_sb = keep.tile([P, PACK], F32, name="gs_sb")
+        nc.sync.dma_start(gs_sb[:], gs.rearrange("(p t) o -> p (t o)", t=PACK))
+        n1_sb = load_list("n1_sb", n1)
+        n3_sb = load_list("n3_sb", n3)
+        n2_sb = load_list("n2_sb", n2)
+        n4_sb = load_list("n4_sb", n4)
+        n5_sb = load_list("n5_sb", n5)
+        n6_sb = load_list("n6_sb", n6)
+
+        plain = [keep.tile([P, WINDOW], F32, name=f"plain{t}") for t in range(PACK)]
+        scaled = [keep.tile([P, WINDOW], F32, name=f"scaled{t}") for t in range(PACK)]
+        nc.vector.memset(plain[0][:, S:], 0.0)
+        nc.vector.memset(scaled[0][:, S:], 0.0)
+
+        factor = keep.tile([P, PACK], F32, name="factor")
+        nc.scalar.mul(factor[:], gs_sb[:], 0.75)
+
+        tok_scales = keep.tile([P, S], U8, name="tok_scales", align_bytes=64)
+        tok_words = keep.tile([P, S], U32, name="tok_words", align_bytes=64)
+        cand_picked = keep.tile([P, C], U8, name="cand_picked", align_bytes=64)
+        cand_scales = keep.tile([P, PACK, P], U8, name="cand_scales", align_bytes=64)
+        cand_words = keep.tile([P, PACK, P], U32, name="cand_words", align_bytes=64)
+        nc.vector.tensor_copy(tok_scales[:], table_scales[:].indirect(offs_sb[:]))
+        nc.vector.tensor_copy(cand_picked[:], table_scales[:].indirect(cand_sb[:]))
+        nc.vector.tensor_copy(cand_scales[:], cand_picked[:].rearrange("p (m t) -> p t m", t=PACK))
+
+        w_grouped = keep.tile([P, PACK, P, PACK], BF16, name="w_grouped", align_bytes=64)
+        for u in range(2):
+            nc.scalar.copy(
+                w_grouped[:, :, u * (P // 2) : (u + 1) * (P // 2), :].rearrange("p t m j -> p m j t"),
+                w_raw[u][:].rearrange("p j (m t) -> p m j t", t=PACK),
+            )
+        w_words = keep.tile([P, PACK, P], U32, name="w_words", align_bytes=64)
+        w_scales = keep.tile([P, PACK, P], U8, name="w_scales", align_bytes=64)
+        nc.vector.quantize_mx(
+            out=w_words[:].rearrange("p t m -> p (t m)").bitcast(FP8X4),
+            scales=w_scales[:].rearrange("p t m -> p (t m)"),
+            in_=w_grouped[:].rearrange("p t m j -> p (t m j)"),
+        )
+
+        def project(t, a, b, acc):
+            nc.tensor.matmul_mx(
+                out=acc[:],
+                lhsT=w_words[:, t, :].bitcast(FP8X4),
+                lhsT_scale=w_scales[:, t, :],
+                rhs=tok_words[:, a:b].bitcast(FP8X4),
+                rhs_scale=tok_scales[:, a:b],
+                start=True,
+                stop=True,
+            )
+            nc.scalar.copy(plain[t][:, a:b], acc[:])
+            return acc
+
+        halves = []
+        for u in range(2):
+            a, b = u * (S // 2), (u + 1) * (S // 2)
+            nc.vector.tensor_copy(tok_words[:, a:b], table_words[:].indirect(offs_sb[:, a // 16 : b // 16]))
+            halves.append((a, b, project(0, a, b, psum_first.tile([P, b - a], F32, name=f"first{a}"))))
+        nc.vector.tensor_copy(cand_words[:].rearrange("p t m -> p m t"), table_words[:].indirect(cand_sb[:]))
+        for a, b, acc in halves:
+            nc.scalar.activation(scaled[0][:, a:b], acc[:], COPY, scale=factor[:, 0:1])
+        for t in range(1, PACK):
+            acc = project(t, 0, S, psum.tile([P, S], F32, name="acc"))
+            nc.scalar.activation(scaled[t][:, :S], acc[:], COPY, scale=factor[:, t : t + 1])
+
+        left = keep.tile([P, PACK, S], F32, name="left")
+        right = keep.tile([P, PACK, S], F32, name="right")
+        for t in range(PACK):
+            y1 = plain[(t + 1) % PACK][:, S:]
+            y3 = scaled[(t + 1) % PACK][:, S:]
+            nc.vector.tensor_copy(y1, plain[t][:].indirect(n1_sb[:]))
+            nc.vector.tensor_copy(y3, plain[t][:].indirect(n3_sb[:]))
+            nc.vector.tensor_tensor(left[:, t, :], scaled[t][:].indirect(n2_sb[:]), y1, MULT)
+            nc.vector.tensor_tensor(right[:, t, :], scaled[t][:].indirect(n4_sb[:]), y3, MULT)
+
+        z_words = keep.tile([P, S], U32, name="z_words", align_bytes=64)
+        z_scales = keep.tile([P, S], U8, name="z_scales", align_bytes=64)
+        z_grouped = []
+        for a, b in Z_CHUNKS:
+            z_tile = keep.tile([P, b - a, PACK], BF16, name=f"z_grouped{a}", align_bytes=64)
+            nc.vector.tensor_tensor(
+                z_tile[:].rearrange("p (c i) t -> p c t i", i=4),
+                left[:, :, a:b].rearrange("p t (c i) -> p c t i", i=4),
+                right[:, :, a:b].rearrange("p t (c i) -> p c t i", i=4),
+                SUBTRACT,
+            )
+            z_grouped.append(z_tile)
+
+        minus_s = [keep.tile([P, S], F32, name=f"minus_s{t}") for t in range(PACK)]
+
+        def scores(t, a, b, acc):
+            nc.tensor.matmul_mx(
+                out=acc[:],
+                lhsT=cand_words[:, t, :].bitcast(FP8X4),
+                lhsT_scale=cand_scales[:, t, :],
+                rhs=z_words[:, a:b].bitcast(FP8X4),
+                rhs_scale=z_scales[:, a:b],
+                start=True,
+                stop=True,
+            )
+            nc.scalar.mul(plain[t][:, a:b], acc[:], -0.03125)
+            nc.scalar.mul(minus_s[t][:, a:b], acc[:], -0.0625)
+
+        for (a, b), z_tile in zip(Z_CHUNKS, z_grouped):
+            nc.vector.quantize_mx(
+                out=z_words[:, a:b].bitcast(FP8X4), scales=z_scales[:, a:b], in_=z_tile[:].rearrange("p c t -> p (c t)")
+            )
+            scores(0, a, b, psum_first.tile([P, b - a], F32, name=f"first{a}"))
+        for t in range(1, PACK):
+            scores(t, 0, S, psum.tile([P, S], F32, name="acc"))
+
+        out_rows = out.rearrange("(p t) j -> p t j", t=PACK)
+        minus_st = [keep.tile([P, S], F32, name=f"minus_st{t}") for t in range(PACK)]
+
+        def first_hop(t):
+            nc.vector.tensor_tensor(scaled[t][:, :S], plain[t][:].indirect(n5_sb[:]), minus_s[t][:], ADD)
+            nc.scalar.copy(minus_st[t][:], scaled[t][:, :S])
+
+        def second_hop(t, a, b):
+            result = keep.tile([P, b - a], F32, name=f"result{t}_{a}")
+            places = n6_sb[:, a // 16 : b // 16]
+            nc.vector.tensor_tensor(result[:], scaled[t][:].indirect(places), minus_st[t][:, a:b], SUBTRACT)
+            nc.sync.dma_start(out_rows[:, t, a:b], result[:])
+
+        first_hop(0)
+        for t in range(1, PACK):
+            first_hop(t)
+            second_hop(t - 1, 0, S)
+        second_hop(PACK - 1, 0, S // 2)
+        second_hop(PACK - 1, S // 2, S)

@@ -20,7 +20,6 @@ COPY = mybir.ActivationFunctionType.Copy
 P = 128
 PACK = 4
 WINDOW = 2 * S
-Z_CHUNKS = ((0, 256), (256, 384), (384, 512))
 
 
 def tile_picked_canddethop_none_p_kernel(
@@ -29,8 +28,7 @@ def tile_picked_canddethop_none_p_kernel(
     nc = tc.nc
     with ExitStack() as ctx:
         keep = ctx.enter_context(tc.tile_pool(name="keep", bufs=1))
-        psum = ctx.enter_context(tc.psum_pool(name="psum", bufs=4))
-        psum_first = ctx.enter_context(tc.psum_pool(name="psum_first", bufs=1))
+        psum = ctx.enter_context(tc.psum_pool(name="psum", bufs=8))
 
         def load_list(name, source):
             tile = keep.tile([P, S // 16], U16, name=name)
@@ -38,14 +36,15 @@ def tile_picked_canddethop_none_p_kernel(
             return tile
 
         table_scales = keep.tile([P, T], U8, name="table_scales", align_bytes=64)
-        nc.vector.memset(table_scales[:].bitcast(I32), 0)
+        nc.vector.memset(table_scales[:, : T // 2].bitcast(I32), 0)
+        nc.gpsimd.memset(table_scales[:, T // 2 :].bitcast(I32), 0)
         offs_sb = load_list("offs_sb", offs)
+        cand_sb = load_list("cand_sb", cand)
         for q in range(4):
             nc.sync.dma_start(
                 table_scales[32 * q : 32 * q + 4, :].bitcast(I32),
                 x_scales[0, 4 * q : 4 * q + 4, :].bitcast(I32),
             )
-        cand_sb = load_list("cand_sb", cand)
         w_rows = w1.rearrange("(p j) c -> p j c", j=PACK)
         w_raw = []
         for u in range(2):
@@ -75,14 +74,13 @@ def tile_picked_canddethop_none_p_kernel(
         tok_words = keep.tile([P, S], U32, name="tok_words", align_bytes=64)
         cand_picked = keep.tile([P, C], U8, name="cand_picked", align_bytes=64)
         cand_scales = keep.tile([P, PACK, P], U8, name="cand_scales", align_bytes=64)
-        cand_words = keep.tile([P, PACK, P], U32, name="cand_words", align_bytes=64)
         nc.vector.tensor_copy(tok_scales[:], table_scales[:].indirect(offs_sb[:]))
         nc.vector.tensor_copy(cand_picked[:], table_scales[:].indirect(cand_sb[:]))
         nc.vector.tensor_copy(cand_scales[:], cand_picked[:].rearrange("p (m t) -> p t m", t=PACK))
 
-        w_grouped = keep.tile([P, PACK, P, PACK], BF16, name="w_grouped", align_bytes=64)
-        for u in range(2):
-            nc.scalar.copy(
+        w_grouped = keep.tile([P, PACK, P, PACK], BF16, name="w_grouped", tag="shared", align_bytes=64)
+        for u, copy in enumerate((nc.scalar.copy, nc.vector.tensor_copy)):
+            copy(
                 w_grouped[:, :, u * (P // 2) : (u + 1) * (P // 2), :].rearrange("p t m j -> p m j t"),
                 w_raw[u][:].rearrange("p j (m t) -> p m j t", t=PACK),
             )
@@ -111,7 +109,8 @@ def tile_picked_canddethop_none_p_kernel(
         for u in range(2):
             a, b = u * (S // 2), (u + 1) * (S // 2)
             nc.vector.tensor_copy(tok_words[:, a:b], table_words[:].indirect(offs_sb[:, a // 16 : b // 16]))
-            halves.append((a, b, project(0, a, b, psum_first.tile([P, b - a], F32, name=f"first{a}"))))
+            halves.append((a, b, project(0, a, b, psum.tile([P, b - a], F32, name="acc"))))
+        cand_words = keep.tile([P, PACK, P], U32, name="cand_words", tag="shared", align_bytes=64)
         nc.vector.tensor_copy(cand_words[:].rearrange("p t m -> p m t"), table_words[:].indirect(cand_sb[:]))
         for a, b, acc in halves:
             nc.scalar.activation(scaled[0][:, a:b], acc[:], COPY, scale=factor[:, 0:1])
@@ -121,30 +120,41 @@ def tile_picked_canddethop_none_p_kernel(
 
         left = keep.tile([P, PACK, S], F32, name="left")
         right = keep.tile([P, PACK, S], F32, name="right")
-        for t in range(PACK):
-            y1 = plain[(t + 1) % PACK][:, S:]
-            y3 = scaled[(t + 1) % PACK][:, S:]
-            nc.vector.tensor_copy(y1, plain[t][:].indirect(n1_sb[:]))
-            nc.vector.tensor_copy(y3, plain[t][:].indirect(n3_sb[:]))
-            nc.vector.tensor_tensor(left[:, t, :], scaled[t][:].indirect(n2_sb[:]), y1, MULT)
-            nc.vector.tensor_tensor(right[:, t, :], scaled[t][:].indirect(n4_sb[:]), y3, MULT)
-
         z_words = keep.tile([P, S], U32, name="z_words", align_bytes=64)
         z_scales = keep.tile([P, S], U8, name="z_scales", align_bytes=64)
-        z_grouped = []
-        for a, b in Z_CHUNKS:
-            z_tile = keep.tile([P, b - a, PACK], BF16, name=f"z_grouped{a}", align_bytes=64)
+        minus_s = [keep.tile([P, S], F32, name=f"minus_s{t}") for t in range(PACK)]
+
+        def spare(t):
+            return plain[(t + 1) % PACK][:, S:], scaled[(t + 1) % PACK][:, S:]
+
+        def fetch(t):
+            y1, y3 = spare(t)
+            nc.vector.tensor_copy(y1, plain[t][:].indirect(n1_sb[:]))
+            nc.vector.tensor_copy(y3, plain[t][:].indirect(n3_sb[:]))
+
+        def multiply(product, places, t, first, a, b):
+            window = scaled[t][:].indirect(places[:, a // 16 : b // 16])
+            nc.vector.tensor_tensor(product[:, t, a:b], window, first[:, a:b], MULT)
+
+        def subtract(a, b):
+            z_grouped = keep.tile([P, b - a, PACK], BF16, name=f"z_grouped{a}", align_bytes=64)
             nc.vector.tensor_tensor(
-                z_tile[:].rearrange("p (c i) t -> p c t i", i=4),
+                z_grouped[:].rearrange("p (c i) t -> p c t i", i=4),
                 left[:, :, a:b].rearrange("p t (c i) -> p c t i", i=4),
                 right[:, :, a:b].rearrange("p t (c i) -> p c t i", i=4),
                 SUBTRACT,
             )
-            z_grouped.append(z_tile)
+            return z_grouped
 
-        minus_s = [keep.tile([P, S], F32, name=f"minus_s{t}") for t in range(PACK)]
+        def quantise(z_grouped, a, b):
+            nc.vector.quantize_mx(
+                out=z_words[:, a:b].bitcast(FP8X4),
+                scales=z_scales[:, a:b],
+                in_=z_grouped[:].rearrange("p c t -> p (c t)"),
+            )
 
-        def scores(t, a, b, acc):
+        def scores(t, a, b, scale_out):
+            acc = psum.tile([P, b - a], F32, name="acc")
             nc.tensor.matmul_mx(
                 out=acc[:],
                 lhsT=cand_words[:, t, :].bitcast(FP8X4),
@@ -154,16 +164,33 @@ def tile_picked_canddethop_none_p_kernel(
                 start=True,
                 stop=True,
             )
-            nc.scalar.mul(plain[t][:, a:b], acc[:], -0.03125)
-            nc.scalar.mul(minus_s[t][:, a:b], acc[:], -0.0625)
+            scale_out(plain[t][:, a:b], acc[:], -0.03125)
+            scale_out(minus_s[t][:, a:b], acc[:], -0.0625)
 
-        for (a, b), z_tile in zip(Z_CHUNKS, z_grouped):
-            nc.vector.quantize_mx(
-                out=z_words[:, a:b].bitcast(FP8X4), scales=z_scales[:, a:b], in_=z_tile[:].rearrange("p c t -> p (c t)")
-            )
-            scores(0, a, b, psum_first.tile([P, b - a], F32, name=f"first{a}"))
+        half, three_quarters = S // 2, 3 * S // 4
+        last = PACK - 1
+        for t in range(last):
+            fetch(t)
+            multiply(left, n2_sb, t, spare(t)[0], 0, S)
+            multiply(right, n4_sb, t, spare(t)[1], 0, S)
+        fetch(last)
+        y1, y3 = spare(last)
+        multiply(left, n2_sb, last, y1, 0, half)
+        multiply(right, n4_sb, last, y3, 0, half)
+        multiply(left, n2_sb, last, y1, half, S)
+        z_first = subtract(0, half)
+        multiply(right, n4_sb, last, y3, half, S)
+        quantise(z_first, 0, half)
+        for t in range(PACK):
+            scores(t, 0, half, nc.scalar.mul)
+        z_third = subtract(half, three_quarters)
+        z_fourth = subtract(three_quarters, S)
+        quantise(z_third, half, three_quarters)
+        scores(0, half, three_quarters, nc.scalar.mul)
+        quantise(z_fourth, three_quarters, S)
+        scores(0, three_quarters, S, nc.vector.tensor_scalar_mul)
         for t in range(1, PACK):
-            scores(t, 0, S, psum.tile([P, S], F32, name="acc"))
+            scores(t, half, S, nc.scalar.mul)
 
         out_rows = out.rearrange("(p t) j -> p t j", t=PACK)
         minus_st = [keep.tile([P, S], F32, name=f"minus_st{t}") for t in range(PACK)]

@@ -1,6 +1,7 @@
 from contextlib import ExitStack
 
 import concourse.mybir as mybir
+from concourse.masks import make_identity
 
 K, T, S, H, C = 512, 2048, 512, 512, 512
 FLOPS = 2 * K * H * S + 2 * K * C * S
@@ -28,6 +29,7 @@ def tile_picked_canddethop_none_p_kernel(
     nc = tc.nc
     with ExitStack() as ctx:
         keep = ctx.enter_context(tc.tile_pool(name="keep", bufs=1))
+        ring = ctx.enter_context(tc.tile_pool(name="ring", bufs=2))
         psum = ctx.enter_context(tc.psum_pool(name="psum", bufs=8))
 
         def load_list(name, source):
@@ -67,6 +69,9 @@ def tile_picked_canddethop_none_p_kernel(
         nc.vector.memset(plain[0][:, S:], 0.0)
         nc.vector.memset(scaled[0][:, S:], 0.0)
 
+        identity = keep.tile([P, P], F32, name="identity")
+        make_identity(nc, identity[:])
+
         factor = keep.tile([P, PACK], F32, name="factor")
         nc.scalar.mul(factor[:], gs_sb[:], 0.75)
 
@@ -79,11 +84,11 @@ def tile_picked_canddethop_none_p_kernel(
         nc.vector.tensor_copy(cand_scales[:], cand_picked[:].rearrange("p (m t) -> p t m", t=PACK))
 
         w_grouped = keep.tile([P, PACK, P, PACK], BF16, name="w_grouped", tag="shared", align_bytes=64)
-        for u, copy in enumerate((nc.scalar.copy, nc.vector.tensor_copy)):
-            copy(
-                w_grouped[:, :, u * (P // 2) : (u + 1) * (P // 2), :].rearrange("p t m j -> p m j t"),
-                w_raw[u][:].rearrange("p j (m t) -> p m j t", t=PACK),
-            )
+        w_target = w_grouped[:].rearrange("p t m j -> p m j t")
+        w_source = [half[:].rearrange("p j (m t) -> p m j t", t=PACK) for half in w_raw]
+        nc.scalar.copy(w_target[:, : P // 2], w_source[0])
+        nc.scalar.copy(w_target[:, P // 2 : 3 * P // 4], w_source[1][:, : P // 4])
+        nc.vector.tensor_copy(w_target[:, 3 * P // 4 :], w_source[1][:, P // 4 :])
         w_words = keep.tile([P, PACK, P], U32, name="w_words", align_bytes=64)
         w_scales = keep.tile([P, PACK, P], U8, name="w_scales", align_bytes=64)
         nc.vector.quantize_mx(
@@ -130,21 +135,46 @@ def tile_picked_canddethop_none_p_kernel(
         def fetch(t):
             y1, y3 = spare(t)
             nc.vector.tensor_copy(y1, plain[t][:].indirect(n1_sb[:]))
-            nc.vector.tensor_copy(y3, plain[t][:].indirect(n3_sb[:]))
+            nc.vector.tensor_scalar(y3, plain[t][:].indirect(n3_sb[:]), -1.0, 0.0, MULT, ADD)
 
         def multiply(product, places, t, first, a, b):
             window = scaled[t][:].indirect(places[:, a // 16 : b // 16])
             nc.vector.tensor_tensor(product[:, t, a:b], window, first[:, a:b], MULT)
 
-        def subtract(a, b):
-            z_grouped = keep.tile([P, b - a, PACK], BF16, name=f"z_grouped{a}", align_bytes=64)
+        half, three_quarters = S // 2, 3 * S // 4
+        last = PACK - 1
+        z_first = keep.tile([P, half, PACK], BF16, name="z_first", align_bytes=64)
+        z_third = keep.tile([P, S // 4, PACK], BF16, name="z_third", align_bytes=64)
+        z_fourth = keep.tile([P, S // 4, PACK], BF16, name="z_fourth", align_bytes=64)
+
+        z_planes = keep.tile([P, PACK, half], BF16, name="z_planes")
+
+        def add_on_tensor(t):
+            turned = psum.tile([P, half], F32, name="acc")
+            for a in range(0, half, P):
+                for product in (left, right):
+                    nc.tensor.matmul(
+                        turned[:, a : a + P],
+                        product[:, t, a : a + P],
+                        identity[:],
+                        start=product is left,
+                        stop=product is right,
+                        is_transpose=True,
+                    )
+            turned_sb = ring.tile([P, half], F32, name="turned_sb")
+            nc.scalar.copy(turned_sb[:], turned[:])
+            back = psum.tile([P, half], F32, name="acc")
+            for a in range(0, half, P):
+                nc.tensor.transpose(back[:, a : a + P], turned_sb[:, a : a + P], identity[:])
+            nc.scalar.copy(z_planes[:, t, :], back[:])
+
+        def add_on_vector(z_grouped, a, b):
             nc.vector.tensor_tensor(
                 z_grouped[:].rearrange("p (c i) t -> p c t i", i=4),
                 left[:, :, a:b].rearrange("p t (c i) -> p c t i", i=4),
                 right[:, :, a:b].rearrange("p t (c i) -> p c t i", i=4),
-                SUBTRACT,
+                ADD,
             )
-            return z_grouped
 
         def quantise(z_grouped, a, b):
             nc.vector.quantize_mx(
@@ -167,30 +197,32 @@ def tile_picked_canddethop_none_p_kernel(
             scale_out(plain[t][:, a:b], acc[:], -0.03125)
             scale_out(minus_s[t][:, a:b], acc[:], -0.0625)
 
-        half, three_quarters = S // 2, 3 * S // 4
-        last = PACK - 1
         for t in range(last):
             fetch(t)
             multiply(left, n2_sb, t, spare(t)[0], 0, S)
             multiply(right, n4_sb, t, spare(t)[1], 0, S)
+            add_on_tensor(t)
         fetch(last)
         y1, y3 = spare(last)
         multiply(left, n2_sb, last, y1, 0, half)
         multiply(right, n4_sb, last, y3, 0, half)
         multiply(left, n2_sb, last, y1, half, S)
-        z_first = subtract(0, half)
+        nc.vector.tensor_tensor(z_planes[:, last, :], left[:, last, :half], right[:, last, :half], ADD)
+        nc.scalar.copy(
+            z_first[:].rearrange("p (c i) t -> p c t i", i=4), z_planes[:].rearrange("p t (c i) -> p c t i", i=4)
+        )
         multiply(right, n4_sb, last, y3, half, S)
+        add_on_vector(z_third, half, three_quarters)
+        add_on_vector(z_fourth, three_quarters, S)
         quantise(z_first, 0, half)
-        for t in range(PACK):
-            scores(t, 0, half, nc.scalar.mul)
-        z_third = subtract(half, three_quarters)
-        z_fourth = subtract(three_quarters, S)
         quantise(z_third, half, three_quarters)
-        scores(0, half, three_quarters, nc.scalar.mul)
         quantise(z_fourth, three_quarters, S)
+        scores(0, 0, S // 4, nc.scalar.mul)
+        scores(0, S // 4, half, nc.vector.tensor_scalar_mul)
+        scores(0, half, three_quarters, nc.scalar.mul)
         scores(0, three_quarters, S, nc.vector.tensor_scalar_mul)
         for t in range(1, PACK):
-            scores(t, half, S, nc.scalar.mul)
+            scores(t, 0, S, nc.scalar.mul)
 
         out_rows = out.rearrange("(p t) j -> p t j", t=PACK)
         minus_st = [keep.tile([P, S], F32, name=f"minus_st{t}") for t in range(PACK)]

@@ -42,17 +42,15 @@ def tile_picked_canddethop_none_p_kernel(
         nc.gpsimd.memset(table_scales[:, T // 2 :].bitcast(I32), 0)
         offs_sb = load_list("offs_sb", offs)
         cand_sb = load_list("cand_sb", cand)
+        w_rows = w1.rearrange("(p j) c -> p j c", j=PACK)
+        w_raw = [keep.tile([P, PACK, H // 2], F32, name=f"w_raw{u}") for u in range(2)]
+        nc.sync.dma_start(w_raw[0][:], w_rows[:, :, : H // 2])
         for q in range(4):
             nc.sync.dma_start(
                 table_scales[32 * q : 32 * q + 4, :].bitcast(I32),
                 x_scales[0, 4 * q : 4 * q + 4, :].bitcast(I32),
             )
-        w_rows = w1.rearrange("(p j) c -> p j c", j=PACK)
-        w_raw = []
-        for u in range(2):
-            half = keep.tile([P, PACK, H // 2], F32, name=f"w_raw{u}")
-            nc.sync.dma_start(half[:], w_rows[:, :, u * (H // 2) : (u + 1) * (H // 2)])
-            w_raw.append(half)
+        nc.sync.dma_start(w_raw[1][:], w_rows[:, :, H // 2 :])
         table_words = keep.tile([P, T], U32, name="table_words", align_bytes=64)
         nc.sync.dma_start(table_words[:].bitcast(I32), x_words[0].rearrange("p n t -> p (n t)").bitcast(I32))
         gs_sb = keep.tile([P, PACK], F32, name="gs_sb")
@@ -76,7 +74,6 @@ def tile_picked_canddethop_none_p_kernel(
         nc.scalar.mul(factor[:], gs_sb[:], 0.75)
 
         tok_scales = keep.tile([P, S], U8, name="tok_scales", align_bytes=64)
-        tok_words = keep.tile([P, S], U32, name="tok_words", align_bytes=64)
         cand_picked = keep.tile([P, C], U8, name="cand_picked", align_bytes=64)
         cand_scales = keep.tile([P, PACK, P], U8, name="cand_scales", align_bytes=64)
         nc.vector.tensor_copy(tok_scales[:], table_scales[:].indirect(offs_sb[:]))
@@ -87,8 +84,7 @@ def tile_picked_canddethop_none_p_kernel(
         w_target = w_grouped[:].rearrange("p t m j -> p m j t")
         w_source = [half[:].rearrange("p j (m t) -> p m j t", t=PACK) for half in w_raw]
         nc.scalar.copy(w_target[:, : P // 2], w_source[0])
-        nc.scalar.copy(w_target[:, P // 2 : 3 * P // 4], w_source[1][:, : P // 4])
-        nc.vector.tensor_copy(w_target[:, 3 * P // 4 :], w_source[1][:, P // 4 :])
+        nc.scalar.copy(w_target[:, P // 2 :], w_source[1])
         w_words = keep.tile([P, PACK, P], U32, name="w_words", align_bytes=64)
         w_scales = keep.tile([P, PACK, P], U8, name="w_scales", align_bytes=64)
         nc.vector.quantize_mx(
@@ -96,6 +92,10 @@ def tile_picked_canddethop_none_p_kernel(
             scales=w_scales[:].rearrange("p t m -> p (t m)"),
             in_=w_grouped[:].rearrange("p t m j -> p (t m j)"),
         )
+
+        picked_words = keep.tile([P, S + C], U32, name="picked_words", tag="shared", align_bytes=64)
+        tok_words = picked_words[:, :S]
+        cand_words = picked_words[:, S:].rearrange("p (t m) -> p t m", t=PACK)
 
         def project(t, a, b, acc):
             nc.tensor.matmul_mx(
@@ -115,8 +115,7 @@ def tile_picked_canddethop_none_p_kernel(
             a, b = u * (S // 2), (u + 1) * (S // 2)
             nc.vector.tensor_copy(tok_words[:, a:b], table_words[:].indirect(offs_sb[:, a // 16 : b // 16]))
             halves.append((a, b, project(0, a, b, psum.tile([P, b - a], F32, name="acc"))))
-        cand_words = keep.tile([P, PACK, P], U32, name="cand_words", tag="shared", align_bytes=64)
-        nc.vector.tensor_copy(cand_words[:].rearrange("p t m -> p m t"), table_words[:].indirect(cand_sb[:]))
+        nc.vector.tensor_copy(cand_words.rearrange("p t m -> p m t"), table_words[:].indirect(cand_sb[:]))
         for a, b, acc in halves:
             nc.scalar.activation(scaled[0][:, a:b], acc[:], COPY, scale=factor[:, 0:1])
         for t in range(1, PACK):

from contextlib import ExitStack

import concourse.mybir as mybir
from concourse.masks import make_identity

K, T, S, H, C = 512, 2048, 512, 512, 512
FLOPS = 2 * K * H * S + 2 * K * C * S

F32 = mybir.dt.float32
BF16 = mybir.dt.bfloat16
I32 = mybir.dt.int32
U32 = mybir.dt.uint32
U16 = mybir.dt.uint16
U8 = mybir.dt.uint8
FP8X4 = mybir.dt.float8_e4m3fn_x4
MULT = mybir.AluOpType.mult
ADD = mybir.AluOpType.add
SUBTRACT = mybir.AluOpType.subtract
COPY = mybir.ActivationFunctionType.Copy

P = 128
PACK = 4
WINDOW = 2 * S


def tile_picked_canddethop_none_p_kernel(
    tc, x_words, x_scales, w1, gs, offs, n1, n2, n3, n4, cand, n5, n6, out
):
    nc = tc.nc
    with ExitStack() as ctx:
        keep = ctx.enter_context(tc.tile_pool(name="keep", bufs=1))
        ring = ctx.enter_context(tc.tile_pool(name="ring", bufs=2))
        psum = ctx.enter_context(tc.psum_pool(name="psum", bufs=8))

        def load_list(name, source):
            tile = keep.tile([P, S // 16], U16, name=name)
            nc.sync.dma_start(tile[:], source)
            return tile

        table_scales = keep.tile([P, T], U8, name="table_scales", align_bytes=64)
        nc.vector.memset(table_scales[:, : T // 2].bitcast(I32), 0)
        nc.gpsimd.memset(table_scales[:, T // 2 :].bitcast(I32), 0)
        offs_sb = load_list("offs_sb", offs)
        cand_sb = load_list("cand_sb", cand)
        w_rows = w1.rearrange("(p j) c -> p j c", j=PACK)
        w_raw = [keep.tile([P, PACK, H // 2], F32, name=f"w_raw{u}") for u in range(2)]
        nc.sync.dma_start(w_raw[0][:], w_rows[:, :, : H // 2])
        for q in range(4):
            nc.sync.dma_start(
                table_scales[32 * q : 32 * q + 4, :].bitcast(I32),
                x_scales[0, 4 * q : 4 * q + 4, :].bitcast(I32),
            )
        nc.sync.dma_start(w_raw[1][:], w_rows[:, :, H // 2 :])
        table_words = keep.tile([P, T], U32, name="table_words", align_bytes=64)
        nc.sync.dma_start(table_words[:].bitcast(I32), x_words[0].rearrange("p n t -> p (n t)").bitcast(I32))
        gs_sb = keep.tile([P, PACK], F32, name="gs_sb")
        nc.sync.dma_start(gs_sb[:], gs.rearrange("(p t) o -> p (t o)", t=PACK))
        n1_sb = load_list("n1_sb", n1)
        n3_sb = load_list("n3_sb", n3)
        n2_sb = load_list("n2_sb", n2)
        n4_sb = load_list("n4_sb", n4)
        n5_sb = load_list("n5_sb", n5)
        n6_sb = load_list("n6_sb", n6)

        plain = [keep.tile([P, WINDOW], F32, name=f"plain{t}") for t in range(PACK)]
        scaled = [keep.tile([P, WINDOW], F32, name=f"scaled{t}") for t in range(PACK)]
        nc.vector.memset(plain[0][:, S:], 0.0)
        nc.vector.memset(scaled[0][:, S:], 0.0)

        identity = keep.tile([P, P], F32, name="identity")
        make_identity(nc, identity[:])

        factor = keep.tile([P, PACK], F32, name="factor")
        nc.scalar.mul(factor[:], gs_sb[:], 0.75)

        tok_scales = keep.tile([P, S], U8, name="tok_scales", align_bytes=64)
        cand_picked = keep.tile([P, C], U8, name="cand_picked", align_bytes=64)
        cand_scales = keep.tile([P, PACK, P], U8, name="cand_scales", align_bytes=64)
        nc.vector.tensor_copy(tok_scales[:], table_scales[:].indirect(offs_sb[:]))
        nc.vector.tensor_copy(cand_picked[:], table_scales[:].indirect(cand_sb[:]))
        nc.vector.tensor_copy(cand_scales[:], cand_picked[:].rearrange("p (m t) -> p t m", t=PACK))

        w_grouped = keep.tile([P, PACK, P, PACK], BF16, name="w_grouped", tag="shared", align_bytes=64)
        w_target = w_grouped[:].rearrange("p t m j -> p m j t")
        w_source = [half[:].rearrange("p j (m t) -> p m j t", t=PACK) for half in w_raw]
        nc.scalar.copy(w_target[:, : P // 2], w_source[0])
        nc.scalar.copy(w_target[:, P // 2 :], w_source[1])
        w_words = keep.tile([P, PACK, P], U32, name="w_words", align_bytes=64)
        w_scales = keep.tile([P, PACK, P], U8, name="w_scales", align_bytes=64)
        nc.vector.quantize_mx(
            out=w_words[:].rearrange("p t m -> p (t m)").bitcast(FP8X4),
            scales=w_scales[:].rearrange("p t m -> p (t m)"),
            in_=w_grouped[:].rearrange("p t m j -> p (t m j)"),
        )

        picked_words = keep.tile([P, S + C], U32, name="picked_words", tag="shared", align_bytes=64)
        tok_words = picked_words[:, :S]
        cand_words = picked_words[:, S:].rearrange("p (t m) -> p t m", t=PACK)

        def project(t, a, b, acc):
            nc.tensor.matmul_mx(
                out=acc[:],
                lhsT=w_words[:, t, :].bitcast(FP8X4),
                lhsT_scale=w_scales[:, t, :],
                rhs=tok_words[:, a:b].bitcast(FP8X4),
                rhs_scale=tok_scales[:, a:b],
                start=True,
                stop=True,
            )
            nc.scalar.copy(plain[t][:, a:b], acc[:])
            return acc

        halves = []
        for u in range(2):
            a, b = u * (S // 2), (u + 1) * (S // 2)
            nc.vector.tensor_copy(tok_words[:, a:b], table_words[:].indirect(offs_sb[:, a // 16 : b // 16]))
            halves.append((a, b, project(0, a, b, psum.tile([P, b - a], F32, name="acc"))))
        nc.vector.tensor_copy(cand_words.rearrange("p t m -> p m t"), table_words[:].indirect(cand_sb[:]))
        for a, b, acc in halves:
            nc.scalar.activation(scaled[0][:, a:b], acc[:], COPY, scale=factor[:, 0:1])
        for t in range(1, PACK):
            acc = project(t, 0, S, psum.tile([P, S], F32, name="acc"))
            nc.scalar.activation(scaled[t][:, :S], acc[:], COPY, scale=factor[:, t : t + 1])

        left = keep.tile([P, PACK, S], F32, name="left")
        right = keep.tile([P, PACK, S], F32, name="right")
        z_words = keep.tile([P, S], U32, name="z_words", align_bytes=64)
        z_scales = keep.tile([P, S], U8, name="z_scales", align_bytes=64)
        minus_s = [keep.tile([P, S], F32, name=f"minus_s{t}") for t in range(PACK)]

        def spare(t):
            return plain[(t + 1) % PACK][:, S:], scaled[(t + 1) % PACK][:, S:]

        def fetch(t):
            y1, y3 = spare(t)
            nc.vector.tensor_copy(y1, plain[t][:].indirect(n1_sb[:]))
            nc.vector.tensor_scalar(y3, plain[t][:].indirect(n3_sb[:]), -1.0, 0.0, MULT, ADD)

        def multiply(product, places, t, first, a, b):
            window = scaled[t][:].indirect(places[:, a // 16 : b // 16])
            nc.vector.tensor_tensor(product[:, t, a:b], window, first[:, a:b], MULT)

        half, three_quarters = S // 2, 3 * S // 4
        last = PACK - 1
        z_first = keep.tile([P, half, PACK], BF16, name="z_first", align_bytes=64)
        z_third = keep.tile([P, S // 4, PACK], BF16, name="z_third", align_bytes=64)
        z_fourth = keep.tile([P, S // 4, PACK], BF16, name="z_fourth", align_bytes=64)

        z_planes = keep.tile([P, PACK, half], BF16, name="z_planes")

        def add_on_tensor(t):
            turned = psum.tile([P, half], F32, name="acc")
            for a in range(0, half, P):
                for product in (left, right):
                    nc.tensor.matmul(
                        turned[:, a : a + P],
                        product[:, t, a : a + P],
                        identity[:],
                        start=product is left,
                        stop=product is right,
                        is_transpose=True,
                    )
            turned_sb = ring.tile([P, half], F32, name="turned_sb")
            nc.scalar.copy(turned_sb[:], turned[:])
            back = psum.tile([P, half], F32, name="acc")
            for a in range(0, half, P):
                nc.tensor.transpose(back[:, a : a + P], turned_sb[:, a : a + P], identity[:])
            nc.scalar.copy(z_planes[:, t, :], back[:])

        def add_on_vector(z_grouped, a, b):
            nc.vector.tensor_tensor(
                z_grouped[:].rearrange("p (c i) t -> p c t i", i=4),
                left[:, :, a:b].rearrange("p t (c i) -> p c t i", i=4),
                right[:, :, a:b].rearrange("p t (c i) -> p c t i", i=4),
                ADD,
            )

        def quantise(z_grouped, a, b):
            nc.vector.quantize_mx(
                out=z_words[:, a:b].bitcast(FP8X4),
                scales=z_scales[:, a:b],
                in_=z_grouped[:].rearrange("p c t -> p (c t)"),
            )

        def scores(t, a, b, scale_out):
            acc = psum.tile([P, b - a], F32, name="acc")
            nc.tensor.matmul_mx(
                out=acc[:],
                lhsT=cand_words[:, t, :].bitcast(FP8X4),
                lhsT_scale=cand_scales[:, t, :],
                rhs=z_words[:, a:b].bitcast(FP8X4),
                rhs_scale=z_scales[:, a:b],
                start=True,
                stop=True,
            )
            scale_out(plain[t][:, a:b], acc[:], -0.03125)
            scale_out(minus_s[t][:, a:b], acc[:], -0.0625)

        for t in range(last):
            fetch(t)
            multiply(left, n2_sb, t, spare(t)[0], 0, S)
            multiply(right, n4_sb, t, spare(t)[1], 0, S)
            add_on_tensor(t)
        fetch(last)
        y1, y3 = spare(last)
        multiply(left, n2_sb, last, y1, 0, half)
        multiply(right, n4_sb, last, y3, 0, half)
        multiply(left, n2_sb, last, y1, half, S)
        nc.vector.tensor_tensor(z_planes[:, last, :], left[:, last, :half], right[:, last, :half], ADD)
        nc.scalar.copy(
            z_first[:].rearrange("p (c i) t -> p c t i", i=4), z_planes[:].rearrange("p t (c i) -> p c t i", i=4)
        )
        multiply(right, n4_sb, last, y3, half, S)
        add_on_vector(z_third, half, three_quarters)
        add_on_vector(z_fourth, three_quarters, S)
        quantise(z_first, 0, half)
        quantise(z_third, half, three_quarters)
        quantise(z_fourth, three_quarters, S)
        scores(0, 0, S // 4, nc.scalar.mul)
        scores(0, S // 4, half, nc.vector.tensor_scalar_mul)
        scores(0, half, three_quarters, nc.scalar.mul)
        scores(0, three_quarters, S, nc.vector.tensor_scalar_mul)
        for t in range(1, PACK):
            scores(t, 0, S, nc.scalar.mul)

        out_rows = out.rearrange("(p t) j -> p t j", t=PACK)
        minus_st = [keep.tile([P, S], F32, name=f"minus_st{t}") for t in range(PACK)]

        def first_hop(t):
            nc.vector.tensor_tensor(scaled[t][:, :S], plain[t][:].indirect(n5_sb[:]), minus_s[t][:], ADD)
            nc.scalar.copy(minus_st[t][:], scaled[t][:, :S])

        def second_hop(t, a, b):
            result = keep.tile([P, b - a], F32, name=f"result{t}_{a}")
            places = n6_sb[:, a // 16 : b // 16]
            nc.vector.tensor_tensor(result[:], scaled[t][:].indirect(places), minus_st[t][:, a:b], SUBTRACT)
            nc.sync.dma_start(out_rows[:, t, a:b], result[:])

        first_hop(0)
        for t in range(1, PACK):
            first_hop(t)
            second_hop(t - 1, 0, S)
        second_hop(PACK - 1, 0, S // 2)
        second_hop(PACK - 1, S // 2, S)
